import numpy as np
import ml_dtypes


def mxq(x, axis, fmt="e4m3"):
    dtype, down = {"e4m3": (ml_dtypes.float8_e4m3fn, 7), "e5m2": (ml_dtypes.float8_e5m2, 14)}[fmt]
    v = np.moveaxis(np.asarray(x, np.float32).astype(ml_dtypes.bfloat16).astype(np.float64), axis, -1)
    blocks = v.reshape(v.shape[:-1] + (-1, 32))
    amax = np.abs(blocks).max(-1, keepdims=True)
    byte = np.maximum(np.where(amax > 0, np.frexp(amax)[1] - 1 + 127, 0) - down, 1)
    scale = np.exp2(byte - 127.0)
    codes = (blocks / scale).astype(np.float32).astype(dtype).astype(np.float64)
    return np.moveaxis((codes * scale).reshape(v.shape), -1, axis)


WIDE = False


def mx_kscale(k):
    if not WIDE:
        return np.ones(k)
    levels = np.array([30, -30])
    if k % 512:
        return np.exp2(np.random.permutation(np.resize(levels, k // 32))).repeat(32)
    a = np.empty((k // 512, 16))
    for p in range(k // 512):
        a[p, :8] = np.random.permutation(np.resize(levels, 8))
        for g in range(8):
            far = levels[np.abs(levels - a[p, g]) >= 10]
            a[p, g + 8] = far[np.random.randint(len(far))]
    return np.exp2(a.ravel()).repeat(32)


def f64(x):
    return np.asarray(x).astype(np.float64)


def striped(idx):
    return np.tile(np.asarray(idx).reshape(-1, 16).T, (8, 1)).astype(np.uint16)


def unstriped(offs):
    return offs[:16].T.reshape(-1).astype(np.int64)


E2M1 = np.array([0.0, 0.5, 1.0, 1.5, 2.0, 3.0, 4.0, 6.0, -0.0, -0.5, -1.0, -1.5, -2.0, -3.0, -4.0, -6.0])


def pack_weight(w, fmt):
    k, n = w.shape
    w = f64(np.asarray(w, np.float32).astype(ml_dtypes.bfloat16)).reshape(k // 32, 32, n)
    amax = np.abs(w).max(1)
    if fmt in ("e4m3", "e5m2"):
        byte = np.frexp(amax)[1] - 1 + 127 - (7 if fmt == "e4m3" else 14)
    else:
        mant, ex = np.frexp(amax / 6.0)
        byte = np.where(mant > 0.5, ex, ex - 1) + 127
    byte = np.clip(np.where(amax > 0, byte, 1), 1, 254)
    scaled = (w * np.exp2(127.0 - byte)[:, None, :]).reshape(k, n).astype(np.float32)
    by_word = np.ascontiguousarray(scaled.reshape(k // 512, 128, 4, n).transpose(0, 1, 3, 2))
    if fmt in ("e4m3", "e5m2"):
        words = by_word.astype(ml_dtypes.float8_e4m3fn if fmt == "e4m3" else ml_dtypes.float8_e5m2).view(np.uint8)
    else:
        c = by_word.astype(ml_dtypes.float4_e2m1fn).view(np.uint8) & 0xF
        words = (c[..., 0::2] | (c[..., 1::2] << 4)).reshape(k // 512, 128, 2 * n)
    return np.ascontiguousarray(words), np.ascontiguousarray(byte.astype(np.uint8).reshape(k // 512, 16, n))


def unpack_weight(words, scales, fmt):
    g, _, n = scales.shape
    words = np.ascontiguousarray(words).reshape(g, 128, n, -1)
    if fmt in ("e4m3", "e5m2"):
        vals = words.view(ml_dtypes.float8_e4m3fn if fmt == "e4m3" else ml_dtypes.float8_e5m2).astype(np.float64)
    else:
        nib = np.empty((g, 128, n, 4), np.uint8)
        nib[..., 0::2] = words & 0xF
        nib[..., 1::2] = words >> 4
        vals = E2M1[nib]
    vals = vals * np.repeat(np.exp2(scales.astype(np.float64) - 127.0), 8, axis=1)[..., None]
    return vals.transpose(0, 1, 3, 2).reshape(g * 512, n)


def sigmoid(v):
    return 1.0 / (1.0 + np.exp(-v))


K, T, Z, J, R, Q, N, L = 512, 1024, 1024, 256, 512, 1024, 256, 512


def setup_inputs():
    n = np.random.standard_normal
    idx = np.random.permutation(T)[:J]
    idx2 = np.random.permutation(Z)[:J]
    idx3 = np.random.permutation(Q)[:J]
    fk = mx_kscale(K)
    fr = mx_kscale(R)
    fl = mx_kscale(L)
    xtp = pack_weight(n((K, T)) / fk[:, None], "e2m1")
    xop = pack_weight(n((K, Z)) / fk[:, None], "e4m3")
    wp = pack_weight(n((K, R)) * 1 / np.sqrt(K) * fk[:, None] * fr, "e4m3")
    w2p = pack_weight(n((K, R)) * 1 / np.sqrt(K) * fk[:, None] * fr, "e5m2")
    wbp = pack_weight(n((R, N)) * 1 / np.sqrt(R) / fr[:, None], "e2m1")
    sxp = pack_weight(n((L, J)) / fl[:, None], "e4m3")
    wsp = pack_weight(n((L, N)) * 1 / np.sqrt(L) * fl[:, None], "e4m3")
    return {
        "xt_words": xtp[0],
        "xt_scales": xtp[1],
        "xo_words": xop[0],
        "xo_scales": xop[1],
        "w_words": wp[0],
        "w_scales": wp[1],
        "w2_words": w2p[0],
        "w2_scales": w2p[1],
        "tg": (1.0 * n((R, Q))).astype(np.float32),
        "sg": (np.random.uniform(0.6, 1.6, (R, 1))).astype(np.float32),
        "bg": (np.random.uniform(-1.0, 1.0, (R, 1))).astype(np.float32),
        "wb_words": wbp[0],
        "wb_scales": wbp[1],
        "sx_words": sxp[0],
        "sx_scales": sxp[1],
        "ws_words": wsp[0],
        "ws_scales": wsp[1],
        "offs": striped(idx),
        "offs2": striped(idx2),
        "offs3": striped(idx3),
    }


def reference(xt_words, xt_scales, xo_words, xo_scales, w_words, w_scales, w2_words, w2_scales, tg, sg, bg, wb_words, wb_scales, sx_words, sx_scales, ws_words, ws_scales, offs, offs2, offs3):
    idx = unstriped(offs)
    idx2 = unstriped(offs2)
    idx3 = unstriped(offs3)
    xtu = unpack_weight(xt_words, xt_scales, "e2m1")
    xou = unpack_weight(xo_words, xo_scales, "e4m3")
    wu = unpack_weight(w_words, w_scales, "e4m3")
    w2u = unpack_weight(w2_words, w2_scales, "e5m2")
    wbu = unpack_weight(wb_words, wb_scales, "e2m1")
    sxu = unpack_weight(sx_words, sx_scales, "e4m3")
    wsu = unpack_weight(ws_words, ws_scales, "e4m3")
    xtidxg = xtu[:, idx]
    xoidx2g = xou[:, idx2]
    a = wu.T @ xtidxg + w2u.T @ xoidx2g
    b = w2u.T @ xtidxg + wu.T @ xoidx2g
    hid = np.maximum(a, b) * sigmoid(f64(tg)[:, idx3] * f64(sg) + f64(bg))
    hidq = mxq(hid, 0, "e5m2")
    y = wbu.T @ hidq + wsu.T @ sxu
    return y

@@ -1,0 +1,195 @@
+from contextlib import ExitStack
+
+import concourse.mybir as mybir
+from concourse.masks import make_identity
+
+K, T, Z, J, R, Q, N, L = 512, 1024, 1024, 256, 512, 1024, 256, 512
+FLOPS = 2 * (4 * K * R * J + R * N * J + L * N * J)
+
+F32 = mybir.dt.float32
+BF16 = mybir.dt.bfloat16
+I32 = mybir.dt.int32
+U32 = mybir.dt.uint32
+U16 = mybir.dt.uint16
+U8 = mybir.dt.uint8
+E4M3 = mybir.dt.float8_e4m3fn_x4
+E5M2 = mybir.dt.float8_e5m2_x4
+E2M1 = mybir.dt.float4_e2m1fn_x4
+ACT = mybir.ActivationFunctionType
+ALU = mybir.AluOpType
+
+P = 128
+PACK = 4
+HALF = 128
+
+
+def tile_list_crossed_tablegate_skip_plain_kernel(
+    tc, xt_words, xt_scales, xo_words, xo_scales, w_words, w_scales, w2_words, w2_scales, tg, sg, bg,
+    wb_words, wb_scales, sx_words, sx_scales, ws_words, ws_scales, offs, offs2, offs3, out,
+):
+    nc = tc.nc
+    halves = J // HALF
+
+    def words(dram):
+        return dram[0].rearrange("p c b -> p (c b)").bitcast(I32)
+
+    def all_partitions(scales):
+        rows, width = scales.shape[1], scales.shape[2] // 4
+        return scales[0].bitcast(I32).unsqueeze(1).to_broadcast([rows, P // rows, width])
+
+    with ExitStack() as ctx:
+        sb = ctx.enter_context(tc.tile_pool(name="sb", bufs=1))
+        ps = ctx.enter_context(tc.psum_pool(name="ps", bufs=1))
+
+        def tile(name, shape, dtype, tag=None):
+            return sb.tile(shape, dtype, name=name, tag=tag or name, align_bytes=64)
+
+        XT_S, XO_S, W_S, W2_S = 0, J, 2 * J, 2 * J + R
+        WB_S = W2_S + R
+        SX_S = WB_S + N
+        WS_S = SX_S + J
+        WIDTH = WS_S + N
+
+        list_t = tile("list_t", [P, J // 16], U16)
+        list_o = tile("list_o", [P, J // 16], U16)
+        list_g = tile("list_g", [P, J // 16], U16)
+        xt_tab = tile("xt_tab", [P, T], U16)
+        xo_tab = tile("xo_tab", [P, Z], U32)
+        xt_stab = tile("xt_stab", [P, T], U8)
+        xo_stab = tile("xo_stab", [P, Z], U8)
+        xt_g = tile("xt_g", [P, J], U16)
+        xo_g = tile("xo_g", [P, J], U32)
+        xt_sg = tile("xt_sg", [P, J], U8)
+        xo_sg = tile("xo_sg", [P, J], U8)
+        w_sb = tile("w_sb", [P, R], U32)
+        w2_sb = tile("w2_sb", [P, R], U32)
+        stage = tile("stage", [P, WIDTH], U8)
+        planes = tile("planes", [P, WIDTH], U8)
+        gate_tab = [tile("gate_tab%d" % t, [P, Q], F32) for t in range(2)]
+        slope = tile("slope", [P, PACK], F32)
+        offset = tile("offset", [P, PACK], F32)
+        gate = tile("gate", [P, PACK, J], F32)
+        ident = tile("ident", [P, P], F32)
+
+        def staged(first, scales):
+            nc.sync.dma_start(
+                out=stage[0:P:8, first : first + scales.shape[2]].bitcast(I32), in_=scales[0].bitcast(I32)
+            )
+
+        tg_rows = tg.rearrange("(p t) q -> t p q", t=PACK)
+        nc.gpsimd.dma_start(out=slope[:], in_=sg.rearrange("(p t) o -> p (t o)", t=PACK))
+        nc.gpsimd.dma_start(out=offset[:], in_=bg.rearrange("(p t) o -> p (t o)", t=PACK))
+        nc.vector.memset(planes[:].bitcast(I32), 0)
+        make_identity(nc, ident[:])
+
+        nc.sync.dma_start(list_t[:], offs)
+        nc.sync.dma_start(out=xt_stab[:].bitcast(I32), in_=all_partitions(xt_scales))
+        nc.sync.dma_start(list_o[:], offs2)
+        nc.sync.dma_start(out=xo_stab[:].bitcast(I32), in_=all_partitions(xo_scales))
+        staged(W_S, w_scales)
+        staged(W2_S, w2_scales)
+        nc.sync.dma_start(out=xt_tab[:].bitcast(I32), in_=xt_words[0].bitcast(I32))
+        nc.sync.dma_start(out=w_sb[:].bitcast(I32), in_=words(w_words))
+        staged(WB_S, wb_scales)
+        staged(SX_S, sx_scales)
+        staged(WS_S, ws_scales)
+        nc.sync.dma_start(list_g[:], offs3)
+        nc.sync.dma_start(out=w2_sb[:].bitcast(I32), in_=words(w2_words))
+        nc.sync.dma_start(out=xo_tab[:].bitcast(I32), in_=words(xo_words))
+        for t in range(2):
+            nc.sync.dma_start(out=gate_tab[t][:], in_=tg_rows[t])
+
+        nc.vector.tensor_copy(xt_sg[:], xt_stab[:].indirect(list_t[:]))
+        nc.vector.tensor_copy(xo_sg[:], xo_stab[:].indirect(list_o[:]))
+        nc.vector.tensor_copy(stage[:, XT_S : XT_S + J].bitcast(I32), xt_sg[:].bitcast(I32))
+        nc.vector.tensor_copy(stage[:, XO_S : XO_S + J].bitcast(I32), xo_sg[:].bitcast(I32))
+        gate_tab.append(tile("gate_tab2", [P, Q], F32, tag="xo_stab"))
+        nc.sync.dma_start(out=gate_tab[2][:], in_=tg_rows[2])
+        for r in range(4):
+            nc.scalar.dma_start(out=planes[r:P:32, :].bitcast(I32), in_=stage[8 * r : P : 32, :].bitcast(I32))
+        nc.vector.tensor_copy(xt_g[:], xt_tab[:].indirect(list_t[:]))
+        nc.vector.tensor_copy(xo_g[:], xo_tab[:].indirect(list_o[:]))
+        gate_tab.append(tile("gate_tab3", [P, Q], F32, tag="xt_tab"))
+        nc.sync.dma_start(out=gate_tab[3][:], in_=tg_rows[3])
+        sx_sb = tile("sx_sb", [P, J], U32, tag="stage")
+        nc.sync.dma_start(out=sx_sb[:].bitcast(I32), in_=words(sx_words))
+        ws_sb = tile("ws_sb", [P, N], U32, tag="xo_tab")
+        nc.sync.dma_start(out=ws_sb[:].bitcast(I32), in_=words(ws_words))
+
+        acc_a = [ps.tile([P, R], F32, name="acc_a%d" % h) for h in range(halves)]
+        acc_b = [ps.tile([P, R], F32, name="acc_b%d" % h) for h in range(halves)]
+        turned = [ps.tile([P, PACK, HALF], F32, name="turned%d" % h) for h in range(halves)]
+        acc_y = [ps.tile([P, J], F32, name="acc_y%d" % u) for u in range(N // P)]
+
+        first = (w_sb[:].bitcast(E4M3), planes[:, W_S : W_S + R])
+        second = (w2_sb[:].bitcast(E5M2), planes[:, W2_S : W2_S + R])
+        for accs, (codes, scales) in ((acc_a, first), (acc_b, second)):
+            for h in range(halves):
+                nc.tensor.matmul_mx(
+                    out=accs[h][:], lhsT=xt_g[:, h * HALF : (h + 1) * HALF].bitcast(E2M1),
+                    lhsT_scale=planes[:, XT_S + h * HALF : XT_S + (h + 1) * HALF],
+                    rhs=codes, rhs_scale=scales, start=True, stop=False,
+                )
+        for accs, (codes, scales) in ((acc_a, second), (acc_b, first)):
+            for h in range(halves):
+                nc.tensor.matmul_mx(
+                    out=accs[h][:], lhsT=xo_g[:, h * HALF : (h + 1) * HALF].bitcast(E4M3),
+                    lhsT_scale=planes[:, XO_S + h * HALF : XO_S + (h + 1) * HALF],
+                    rhs=codes, rhs_scale=scales, start=False, stop=True,
+                )
+
+        def look(t):
+            nc.scalar.activation(
+                out=gate[:, t, :], in_=gate_tab[t][:].indirect(list_g[:]), func=ACT.Sigmoid,
+                bias=offset[:, t : t + 1], scale=slope[:, t : t + 1],
+            )
+
+        look(0)
+        wb_sb = tile("wb_sb", [P, 2 * N], U8, tag="gate_tab0")
+        nc.sync.dma_start(out=wb_sb[:].bitcast(I32), in_=wb_words[0].bitcast(I32))
+        look(1)
+        a_sb = [sb.tile([P, PACK, P], F32, name="a_sb%d" % h) for h in range(halves)]
+        larger = [sb.tile([P, PACK, P], F32, name="larger%d" % h) for h in range(halves)]
+        for h in range(halves):
+            nc.scalar.copy(out=a_sb[h][:], in_=acc_a[h][:].rearrange("j (p t) -> j t p", t=PACK))
+        look(2)
+        look(3)
+        for h in range(halves):
+            nc.vector.tensor_tensor(
+                out=larger[h][:], in0=acc_b[h][:].rearrange("j (p t) -> j t p", t=PACK), in1=a_sb[h][:], op=ALU.max
+            )
+            for t in range(PACK):
+                nc.tensor.transpose(turned[h][:, t, :], larger[h][:, t, :], ident[:])
+
+        for u in range(N // P):
+            nc.tensor.matmul_mx(
+                out=acc_y[u][:], lhsT=ws_sb[:, u * P : (u + 1) * P].bitcast(E4M3),
+                lhsT_scale=planes[:, WS_S + u * P : WS_S + (u + 1) * P],
+                rhs=sx_sb[:].bitcast(E4M3), rhs_scale=planes[:, SX_S : SX_S + J], start=True, stop=False,
+            )
+
+        hid = [sb.tile([P, HALF, PACK], BF16, name="hid%d" % h, align_bytes=64) for h in range(halves)]
+        hid_q = [sb.tile([P, HALF], U32, name="hid_q%d" % h, align_bytes=64) for h in range(halves)]
+        hid_s = [sb.tile([P, HALF], U8, name="hid_s%d" % h, align_bytes=64) for h in range(halves)]
+        for h in range(halves):
+            nc.vector.tensor_tensor(
+                out=hid[h][:], in0=turned[h][:].rearrange("p t j -> p j t"),
+                in1=gate[:, :, h * HALF : (h + 1) * HALF].rearrange("p t j -> p j t"), op=ALU.mult,
+            )
+        for h in range(halves):
+            nc.vector.quantize_mx(
+                out=hid_q[h][:].bitcast(E5M2), scales=hid_s[h][:], in_=hid[h][:].rearrange("p j t -> p (j t)")
+            )
+            for u in range(N // P):
+                nc.tensor.matmul_mx(
+                    out=acc_y[u][:, h * HALF : (h + 1) * HALF],
+                    lhsT=wb_sb[:, 2 * u * P : 2 * (u + 1) * P].bitcast(E2M1),
+                    lhsT_scale=planes[:, WB_S + u * P : WB_S + (u + 1) * P],
+                    rhs=hid_q[h][:].bitcast(E5M2), rhs_scale=hid_s[h][:], start=False, stop=(h == halves - 1),
+                )
+
+        y_sb = [sb.tile([P, J], F32, name="y_sb%d" % u) for u in range(N // P)]
+        nc.scalar.copy(out=y_sb[0][:], in_=acc_y[0][:])
+        nc.scalar.dma_start(out=out[0:P, :], in_=y_sb[0][:])
+        nc.vector.tensor_copy(out=y_sb[1][:], in_=acc_y[1][:])
+        nc.sync.dma_start(out=out[P : 2 * P, :], in_=y_sb[1][:])

@@ -33,10 +33,6 @@ def tile_list_crossed_tablegate_skip_plain_kernel(
     def words(dram):
         return dram[0].rearrange("p c b -> p (c b)").bitcast(I32)
 
-    def all_partitions(scales):
-        rows, width = scales.shape[1], scales.shape[2] // 4
-        return scales[0].bitcast(I32).unsqueeze(1).to_broadcast([rows, P // rows, width])
-
     with ExitStack() as ctx:
         sb = ctx.enter_context(tc.tile_pool(name="sb", bufs=1))
         ps = ctx.enter_context(tc.psum_pool(name="ps", bufs=1))
@@ -44,20 +40,21 @@ def tile_list_crossed_tablegate_skip_plain_kernel(
         def tile(name, shape, dtype, tag=None):
             return sb.tile(shape, dtype, name=name, tag=tag or name, align_bytes=64)
 
-        XT_S, XO_S, W_S, W2_S = 0, J, 2 * J, 2 * J + R
-        WB_S = W2_S + R
-        SX_S = WB_S + N
-        WS_S = SX_S + J
-        WIDTH = WS_S + N
+        shared = ctx.enter_context(tc.tile_pool(name="shared", bufs=1))
+
+        def tenant(name, shape, dtype, at=0):
+            return shared.tile(shape, dtype, name=name, align_bytes=64, offset=at)
+
+        XT_S, XO_S, W_S, W2_S, WIDTH = 0, J, 2 * J, 2 * J + R, 2 * J + 2 * R
+        WB_S, SX_S, WS_S, WIDTH2 = 0, N, N + J, 2 * N + J
 
         list_t = tile("list_t", [P, J // 16], U16)
         list_o = tile("list_o", [P, J // 16], U16)
         list_g = tile("list_g", [P, J // 16], U16)
-        xt_tab = tile("xt_tab", [P, T], U16)
-        xo_tab = tile("xo_tab", [P, Z], U32)
+        xt_tab = tenant("xt_tab", [P, T], U16, at=3072)
+        xo_tab = tenant("xo_tab", [P, Z], U32, at=8192)
         xt_stab = tile("xt_stab", [P, T], U8)
         xo_stab = tile("xo_stab", [P, Z], U8)
-        xt_g = tile("xt_g", [P, J], U16)
         xo_g = tile("xo_g", [P, J], U32)
         xt_sg = tile("xt_sg", [P, J], U8)
         xo_sg = tile("xo_sg", [P, J], U8)
@@ -65,56 +62,61 @@ def tile_list_crossed_tablegate_skip_plain_kernel(
         w2_sb = tile("w2_sb", [P, R], U32)
         stage = tile("stage", [P, WIDTH], U8)
         planes = tile("planes", [P, WIDTH], U8)
-        gate_tab = [tile("gate_tab%d" % t, [P, Q], F32) for t in range(2)]
+        stage2 = tile("stage2", [P, WIDTH2], U8)
+        gate_tab = [tile("gate_tab0", [P, Q], F32)]
         slope = tile("slope", [P, PACK], F32)
         offset = tile("offset", [P, PACK], F32)
         gate = tile("gate", [P, PACK, J], F32)
         ident = tile("ident", [P, P], F32)
 
-        def staged(first, scales):
-            nc.sync.dma_start(
-                out=stage[0:P:8, first : first + scales.shape[2]].bitcast(I32), in_=scales[0].bitcast(I32)
-            )
+        def load_rows(queue, into, first, scales):
+            queue.dma_start(out=into[0:P:8, first : first + scales.shape[2]].bitcast(I32), in_=scales[0].bitcast(I32))
+
+        def load_window(window, scales):
+            rows, width = scales.shape[1], scales.shape[2] // 4
+            source = scales[0].bitcast(I32).unsqueeze(1).to_broadcast([rows, P // rows, width])
+            nc.sync.dma_start(out=window[:].bitcast(I32), in_=source)
+
+        def spread(queue, into, rows):
+            for first in range(0, P, 32):
+                queue.dma_start(
+                    out=into[first : first + 4, :].bitcast(I32), in_=rows[first : first + 32 : 8, :].bitcast(I32)
+                )
 
         tg_rows = tg.rearrange("(p t) q -> t p q", t=PACK)
+        nc.vector.memset(planes[:].bitcast(I32), 0)
         nc.gpsimd.dma_start(out=slope[:], in_=sg.rearrange("(p t) o -> p (t o)", t=PACK))
         nc.gpsimd.dma_start(out=offset[:], in_=bg.rearrange("(p t) o -> p (t o)", t=PACK))
-        nc.vector.memset(planes[:].bitcast(I32), 0)
         make_identity(nc, ident[:])
+        load_rows(nc.gpsimd, stage2, WB_S, wb_scales)
+        load_rows(nc.gpsimd, stage2, SX_S, sx_scales)
+        load_rows(nc.gpsimd, stage2, WS_S, ws_scales)
 
         nc.sync.dma_start(list_t[:], offs)
-        nc.sync.dma_start(out=xt_stab[:].bitcast(I32), in_=all_partitions(xt_scales))
+        load_window(xt_stab, xt_scales)
         nc.sync.dma_start(list_o[:], offs2)
-        nc.sync.dma_start(out=xo_stab[:].bitcast(I32), in_=all_partitions(xo_scales))
-        staged(W_S, w_scales)
-        staged(W2_S, w2_scales)
+        load_window(xo_stab, xo_scales)
+        load_rows(nc.sync, stage, W_S, w_scales)
+        load_rows(nc.sync, stage, W2_S, w2_scales)
         nc.sync.dma_start(out=xt_tab[:].bitcast(I32), in_=xt_words[0].bitcast(I32))
-        nc.sync.dma_start(out=w_sb[:].bitcast(I32), in_=words(w_words))
-        staged(WB_S, wb_scales)
-        staged(SX_S, sx_scales)
-        staged(WS_S, ws_scales)
+        nc.sync.dma_start(out=gate_tab[0][:], in_=tg_rows[0])
         nc.sync.dma_start(list_g[:], offs3)
-        nc.sync.dma_start(out=w2_sb[:].bitcast(I32), in_=words(w2_words))
+        nc.sync.dma_start(out=w_sb[:].bitcast(I32), in_=words(w_words))
         nc.sync.dma_start(out=xo_tab[:].bitcast(I32), in_=words(xo_words))
-        for t in range(2):
-            nc.sync.dma_start(out=gate_tab[t][:], in_=tg_rows[t])
+        nc.sync.dma_start(out=w2_sb[:].bitcast(I32), in_=words(w2_words))
 
         nc.vector.tensor_copy(xt_sg[:], xt_stab[:].indirect(list_t[:]))
         nc.vector.tensor_copy(xo_sg[:], xo_stab[:].indirect(list_o[:]))
         nc.vector.tensor_copy(stage[:, XT_S : XT_S + J].bitcast(I32), xt_sg[:].bitcast(I32))
         nc.vector.tensor_copy(stage[:, XO_S : XO_S + J].bitcast(I32), xo_sg[:].bitcast(I32))
-        gate_tab.append(tile("gate_tab2", [P, Q], F32, tag="xo_stab"))
-        nc.sync.dma_start(out=gate_tab[2][:], in_=tg_rows[2])
-        for r in range(4):
-            nc.scalar.dma_start(out=planes[r:P:32, :].bitcast(I32), in_=stage[8 * r : P : 32, :].bitcast(I32))
+        spread(nc.scalar, planes, stage)
+        xt_g = tile("xt_g", [P, J], U16, tag="xo_sg")
         nc.vector.tensor_copy(xt_g[:], xt_tab[:].indirect(list_t[:]))
         nc.vector.tensor_copy(xo_g[:], xo_tab[:].indirect(list_o[:]))
-        gate_tab.append(tile("gate_tab3", [P, Q], F32, tag="xt_tab"))
-        nc.sync.dma_start(out=gate_tab[3][:], in_=tg_rows[3])
-        sx_sb = tile("sx_sb", [P, J], U32, tag="stage")
-        nc.sync.dma_start(out=sx_sb[:].bitcast(I32), in_=words(sx_words))
-        ws_sb = tile("ws_sb", [P, N], U32, tag="xo_tab")
-        nc.sync.dma_start(out=ws_sb[:].bitcast(I32), in_=words(ws_words))
+        for t in range(1, PACK):
+            gate_tab.append(tenant("gate_tab%d" % t, [P, Q], F32, at=4096 * (t - 1)))
+        for t in range(1, PACK):
+            nc.sync.dma_start(out=gate_tab[t][:], in_=tg_rows[t])
 
         acc_a = [ps.tile([P, R], F32, name="acc_a%d" % h) for h in range(halves)]
         acc_b = [ps.tile([P, R], F32, name="acc_b%d" % h) for h in range(halves)]
@@ -123,20 +125,27 @@ def tile_list_crossed_tablegate_skip_plain_kernel(
 
         first = (w_sb[:].bitcast(E4M3), planes[:, W_S : W_S + R])
         second = (w2_sb[:].bitcast(E5M2), planes[:, W2_S : W2_S + R])
-        for accs, (codes, scales) in ((acc_a, first), (acc_b, second)):
-            for h in range(halves):
-                nc.tensor.matmul_mx(
-                    out=accs[h][:], lhsT=xt_g[:, h * HALF : (h + 1) * HALF].bitcast(E2M1),
-                    lhsT_scale=planes[:, XT_S + h * HALF : XT_S + (h + 1) * HALF],
-                    rhs=codes, rhs_scale=scales, start=True, stop=False,
-                )
-        for accs, (codes, scales) in ((acc_a, second), (acc_b, first)):
-            for h in range(halves):
-                nc.tensor.matmul_mx(
-                    out=accs[h][:], lhsT=xo_g[:, h * HALF : (h + 1) * HALF].bitcast(E4M3),
-                    lhsT_scale=planes[:, XO_S + h * HALF : XO_S + (h + 1) * HALF],
-                    rhs=codes, rhs_scale=scales, start=False, stop=True,
-                )
+        token = [
+            (xt_g[:, h * HALF : (h + 1) * HALF].bitcast(E2M1), planes[:, XT_S + h * HALF : XT_S + (h + 1) * HALF])
+            for h in range(halves)
+        ]
+        note = [
+            (xo_g[:, h * HALF : (h + 1) * HALF].bitcast(E4M3), planes[:, XO_S + h * HALF : XO_S + (h + 1) * HALF])
+            for h in range(halves)
+        ]
+
+        def product(acc, slots, weight, opens):
+            nc.tensor.matmul_mx(
+                out=acc[:], lhsT=slots[0], lhsT_scale=slots[1], rhs=weight[0], rhs_scale=weight[1],
+                start=opens, stop=not opens,
+            )
+
+        for h in range(halves):
+            product(acc_a[h], token[h], first, True)
+        for h in range(halves):
+            product(acc_b[h], token[h], second, True)
+            product(acc_a[h], note[h], second, False)
+            product(acc_b[h], note[h], first, False)
 
         def look(t):
             nc.scalar.activation(
@@ -145,9 +154,16 @@ def tile_list_crossed_tablegate_skip_plain_kernel(
             )
 
         look(0)
-        wb_sb = tile("wb_sb", [P, 2 * N], U8, tag="gate_tab0")
-        nc.sync.dma_start(out=wb_sb[:].bitcast(I32), in_=wb_words[0].bitcast(I32))
         look(1)
+        ws_sb = tenant("ws_sb", [P, N], U32, at=0)
+        sx_sb = tenant("sx_sb", [P, J], U32, at=1024)
+        wb_sb = tenant("wb_sb", [P, 2 * N], U8, at=2048)
+        planes2 = tenant("planes2", [P, WIDTH2], U8, at=3072)
+        nc.vector.memset(planes2[:].bitcast(I32), 0)
+        nc.sync.dma_start(out=ws_sb[:].bitcast(I32), in_=words(ws_words))
+        nc.sync.dma_start(out=sx_sb[:].bitcast(I32), in_=words(sx_words))
+        nc.sync.dma_start(out=wb_sb[:].bitcast(I32), in_=wb_words[0].bitcast(I32))
+        spread(nc.sync, planes2, stage2)
         a_sb = [sb.tile([P, PACK, P], F32, name="a_sb%d" % h) for h in range(halves)]
         larger = [sb.tile([P, PACK, P], F32, name="larger%d" % h) for h in range(halves)]
         for h in range(halves):
@@ -164,8 +180,8 @@ def tile_list_crossed_tablegate_skip_plain_kernel(
         for u in range(N // P):
             nc.tensor.matmul_mx(
                 out=acc_y[u][:], lhsT=ws_sb[:, u * P : (u + 1) * P].bitcast(E4M3),
-                lhsT_scale=planes[:, WS_S + u * P : WS_S + (u + 1) * P],
-                rhs=sx_sb[:].bitcast(E4M3), rhs_scale=planes[:, SX_S : SX_S + J], start=True, stop=False,
+                lhsT_scale=planes2[:, WS_S + u * P : WS_S + (u + 1) * P],
+                rhs=sx_sb[:].bitcast(E4M3), rhs_scale=planes2[:, SX_S : SX_S + J], start=True, stop=False,
             )
 
         hid = [sb.tile([P, HALF, PACK], BF16, name="hid%d" % h, align_bytes=64) for h in range(halves)]
@@ -184,7 +200,7 @@ def tile_list_crossed_tablegate_skip_plain_kernel(
                 nc.tensor.matmul_mx(
                     out=acc_y[u][:, h * HALF : (h + 1) * HALF],
                     lhsT=wb_sb[:, 2 * u * P : 2 * (u + 1) * P].bitcast(E2M1),
-                    lhsT_scale=planes[:, WB_S + u * P : WB_S + (u + 1) * P],
+                    lhsT_scale=planes2[:, WB_S + u * P : WB_S + (u + 1) * P],
                     rhs=hid_q[h][:].bitcast(E5M2), rhs_scale=hid_s[h][:], start=False, stop=(h == halves - 1),
                 )
 

@@ -60,10 +60,9 @@ def tile_list_crossed_tablegate_skip_plain_kernel(
         xo_sg = tile("xo_sg", [P, J], U8)
         w_sb = tile("w_sb", [P, R], U32)
         w2_sb = tile("w2_sb", [P, R], U32)
-        stage = tile("stage", [P, WIDTH], U8)
         planes = tile("planes", [P, WIDTH], U8)
-        stage2 = tile("stage2", [P, WIDTH2], U8)
-        gate_tab = [tile("gate_tab0", [P, Q], F32)]
+        planes2 = tile("planes2", [P, WIDTH2], U8)
+        gate_tab = [tenant("gate_tab0", [P, Q], F32, at=12288)]
         slope = tile("slope", [P, PACK], F32)
         offset = tile("offset", [P, PACK], F32)
         gate = tile("gate", [P, PACK, J], F32)
@@ -77,27 +76,26 @@ def tile_list_crossed_tablegate_skip_plain_kernel(
             source = scales[0].bitcast(I32).unsqueeze(1).to_broadcast([rows, P // rows, width])
             nc.sync.dma_start(out=window[:].bitcast(I32), in_=source)
 
-        def spread(queue, into, rows):
-            for first in range(0, P, 32):
-                queue.dma_start(
-                    out=into[first : first + 4, :].bitcast(I32), in_=rows[first : first + 32 : 8, :].bitcast(I32)
-                )
+        def spread(queue, rows):
+            for r in range(1, 4):
+                queue.dma_start(out=rows[r:P:32, :].bitcast(I32), in_=rows[8 * r : P : 32, :].bitcast(I32))
 
         tg_rows = tg.rearrange("(p t) q -> t p q", t=PACK)
-        nc.vector.memset(planes[:].bitcast(I32), 0)
+        nc.gpsimd.memset(planes[:, W_S:].bitcast(I32), 0)
+        nc.vector.memset(planes2[:].bitcast(I32), 0)
         nc.gpsimd.dma_start(out=slope[:], in_=sg.rearrange("(p t) o -> p (t o)", t=PACK))
         nc.gpsimd.dma_start(out=offset[:], in_=bg.rearrange("(p t) o -> p (t o)", t=PACK))
+        load_rows(nc.gpsimd, planes2, WB_S, wb_scales)
+        load_rows(nc.gpsimd, planes2, SX_S, sx_scales)
+        load_rows(nc.gpsimd, planes2, WS_S, ws_scales)
         make_identity(nc, ident[:])
-        load_rows(nc.gpsimd, stage2, WB_S, wb_scales)
-        load_rows(nc.gpsimd, stage2, SX_S, sx_scales)
-        load_rows(nc.gpsimd, stage2, WS_S, ws_scales)
 
         nc.sync.dma_start(list_t[:], offs)
         load_window(xt_stab, xt_scales)
         nc.sync.dma_start(list_o[:], offs2)
         load_window(xo_stab, xo_scales)
-        load_rows(nc.sync, stage, W_S, w_scales)
-        load_rows(nc.sync, stage, W2_S, w2_scales)
+        load_rows(nc.sync, planes, W_S, w_scales)
+        load_rows(nc.sync, planes, W2_S, w2_scales)
         nc.sync.dma_start(out=xt_tab[:].bitcast(I32), in_=xt_words[0].bitcast(I32))
         nc.sync.dma_start(out=gate_tab[0][:], in_=tg_rows[0])
         nc.sync.dma_start(list_g[:], offs3)
@@ -107,9 +105,9 @@ def tile_list_crossed_tablegate_skip_plain_kernel(
 
         nc.vector.tensor_copy(xt_sg[:], xt_stab[:].indirect(list_t[:]))
         nc.vector.tensor_copy(xo_sg[:], xo_stab[:].indirect(list_o[:]))
-        nc.vector.tensor_copy(stage[:, XT_S : XT_S + J].bitcast(I32), xt_sg[:].bitcast(I32))
-        nc.vector.tensor_copy(stage[:, XO_S : XO_S + J].bitcast(I32), xo_sg[:].bitcast(I32))
-        spread(nc.scalar, planes, stage)
+        nc.vector.tensor_copy(planes[:, XT_S : XT_S + J].bitcast(I32), xt_sg[:].bitcast(I32))
+        nc.vector.tensor_copy(planes[:, XO_S : XO_S + J].bitcast(I32), xo_sg[:].bitcast(I32))
+        spread(nc.scalar, planes)
         xt_g = tile("xt_g", [P, J], U16, tag="xo_sg")
         nc.vector.tensor_copy(xt_g[:], xt_tab[:].indirect(list_t[:]))
         nc.vector.tensor_copy(xo_g[:], xo_tab[:].indirect(list_o[:]))
@@ -121,7 +119,6 @@ def tile_list_crossed_tablegate_skip_plain_kernel(
         acc_a = [ps.tile([P, R], F32, name="acc_a%d" % h) for h in range(halves)]
         acc_b = [ps.tile([P, R], F32, name="acc_b%d" % h) for h in range(halves)]
         turned = [ps.tile([P, PACK, HALF], F32, name="turned%d" % h) for h in range(halves)]
-        acc_y = [ps.tile([P, J], F32, name="acc_y%d" % u) for u in range(N // P)]
 
         first = (w_sb[:].bitcast(E4M3), planes[:, W_S : W_S + R])
         second = (w2_sb[:].bitcast(E5M2), planes[:, W2_S : W2_S + R])
@@ -154,16 +151,14 @@ def tile_list_crossed_tablegate_skip_plain_kernel(
             )
 
         look(0)
-        look(1)
-        ws_sb = tenant("ws_sb", [P, N], U32, at=0)
-        sx_sb = tenant("sx_sb", [P, J], U32, at=1024)
-        wb_sb = tenant("wb_sb", [P, 2 * N], U8, at=2048)
-        planes2 = tenant("planes2", [P, WIDTH2], U8, at=3072)
-        nc.vector.memset(planes2[:].bitcast(I32), 0)
+        ws_sb = tenant("ws_sb", [P, N], U32, at=12288)
+        sx_sb = tenant("sx_sb", [P, J], U32, at=12288 + 1024)
+        wb_sb = tenant("wb_sb", [P, 2 * N], U8, at=12288 + 2048)
         nc.sync.dma_start(out=ws_sb[:].bitcast(I32), in_=words(ws_words))
         nc.sync.dma_start(out=sx_sb[:].bitcast(I32), in_=words(sx_words))
         nc.sync.dma_start(out=wb_sb[:].bitcast(I32), in_=wb_words[0].bitcast(I32))
-        spread(nc.sync, planes2, stage2)
+        spread(nc.sync, planes2)
+        look(1)
         a_sb = [sb.tile([P, PACK, P], F32, name="a_sb%d" % h) for h in range(halves)]
         larger = [sb.tile([P, PACK, P], F32, name="larger%d" % h) for h in range(halves)]
         for h in range(halves):
@@ -171,18 +166,27 @@ def tile_list_crossed_tablegate_skip_plain_kernel(
         look(2)
         look(3)
         for h in range(halves):
-            nc.vector.tensor_tensor(
-                out=larger[h][:], in0=acc_b[h][:].rearrange("j (p t) -> j t p", t=PACK), in1=a_sb[h][:], op=ALU.max
-            )
+            b_rows = acc_b[h][:].rearrange("j (p t) -> j t p", t=PACK)
+            for pair in range(0, PACK, 2):
+                nc.vector.tensor_tensor(
+                    out=larger[h][:, pair : pair + 2, :], in0=b_rows[:, pair : pair + 2, :],
+                    in1=a_sb[h][:, pair : pair + 2, :], op=ALU.max,
+                )
             for t in range(PACK):
                 nc.tensor.transpose(turned[h][:, t, :], larger[h][:, t, :], ident[:])
 
-        for u in range(N // P):
-            nc.tensor.matmul_mx(
-                out=acc_y[u][:], lhsT=ws_sb[:, u * P : (u + 1) * P].bitcast(E4M3),
-                lhsT_scale=planes2[:, WS_S + u * P : WS_S + (u + 1) * P],
-                rhs=sx_sb[:].bitcast(E4M3), rhs_scale=planes2[:, SX_S : SX_S + J], start=True, stop=False,
-            )
+        acc_y = [
+            [ps.tile([P, HALF], F32, name="acc_y0%d" % u) for u in range(N // P)],
+            [ps.tile([P, HALF], F32, name="acc_y1%d" % u, tag="acc_a%d" % u) for u in range(N // P)],
+        ]
+        for h in range(halves):
+            for u in range(N // P):
+                nc.tensor.matmul_mx(
+                    out=acc_y[h][u][:], lhsT=ws_sb[:, u * P : (u + 1) * P].bitcast(E4M3),
+                    lhsT_scale=planes2[:, WS_S + u * P : WS_S + (u + 1) * P],
+                    rhs=sx_sb[:, h * HALF : (h + 1) * HALF].bitcast(E4M3),
+                    rhs_scale=planes2[:, SX_S + h * HALF : SX_S + (h + 1) * HALF], start=True, stop=False,
+                )
 
         hid = [sb.tile([P, HALF, PACK], BF16, name="hid%d" % h, align_bytes=64) for h in range(halves)]
         hid_q = [sb.tile([P, HALF], U32, name="hid_q%d" % h, align_bytes=64) for h in range(halves)]
@@ -198,14 +202,20 @@ def tile_list_crossed_tablegate_skip_plain_kernel(
             )
             for u in range(N // P):
                 nc.tensor.matmul_mx(
-                    out=acc_y[u][:, h * HALF : (h + 1) * HALF],
+                    out=acc_y[h][u][:],
                     lhsT=wb_sb[:, 2 * u * P : 2 * (u + 1) * P].bitcast(E2M1),
                     lhsT_scale=planes2[:, WB_S + u * P : WB_S + (u + 1) * P],
-                    rhs=hid_q[h][:].bitcast(E5M2), rhs_scale=hid_s[h][:], start=False, stop=(h == halves - 1),
+                    rhs=hid_q[h][:].bitcast(E5M2), rhs_scale=hid_s[h][:], start=False, stop=True,
                 )
 
-        y_sb = [sb.tile([P, J], F32, name="y_sb%d" % u) for u in range(N // P)]
-        nc.scalar.copy(out=y_sb[0][:], in_=acc_y[0][:])
-        nc.scalar.dma_start(out=out[0:P, :], in_=y_sb[0][:])
-        nc.vector.tensor_copy(out=y_sb[1][:], in_=acc_y[1][:])
-        nc.sync.dma_start(out=out[P : 2 * P, :], in_=y_sb[1][:])
+        for h in range(halves):
+            cols = slice(h * HALF, (h + 1) * HALF)
+            y_top = sb.tile([P, HALF], F32, name="y_top%d" % h)
+            nc.scalar.copy(out=y_top[:], in_=acc_y[h][0][:])
+            nc.scalar.dma_start(out=out[0:P, cols], in_=y_top[:])
+            y_low = sb.tile([P, HALF], F32, name="y_low%d" % h)
+            if h == halves - 1:
+                nc.vector.tensor_copy(out=y_low[:], in_=acc_y[h][1][:])
+            else:
+                nc.scalar.copy(out=y_low[:], in_=acc_y[h][1][:])
+            nc.sync.dma_start(out=out[P : 2 * P, cols], in_=y_low[:])

@@ -51,8 +51,8 @@ def tile_list_crossed_tablegate_skip_plain_kernel(
         list_t = tile("list_t", [P, J // 16], U16)
         list_o = tile("list_o", [P, J // 16], U16)
         list_g = tile("list_g", [P, J // 16], U16)
-        xt_tab = tenant("xt_tab", [P, T], U16, at=3072)
-        xo_tab = tenant("xo_tab", [P, Z], U32, at=8192)
+        xt_tab = tenant("xt_tab", [P, T], U16, at=3584)
+        xo_tab = tenant("xo_tab", [P, Z], U32, at=8960)
         xt_stab = tile("xt_stab", [P, T], U8)
         xo_stab = tile("xo_stab", [P, Z], U8)
         xo_g = tile("xo_g", [P, J], U32)
@@ -61,8 +61,7 @@ def tile_list_crossed_tablegate_skip_plain_kernel(
         w_sb = tile("w_sb", [P, R], U32)
         w2_sb = tile("w2_sb", [P, R], U32)
         planes = tile("planes", [P, WIDTH], U8)
-        planes2 = tile("planes2", [P, WIDTH2], U8)
-        gate_tab = [tenant("gate_tab0", [P, Q], F32, at=12288)]
+        gate_tab = [tenant("gate_tab0", [P, Q], F32, at=13056)]
         slope = tile("slope", [P, PACK], F32)
         offset = tile("offset", [P, PACK], F32)
         gate = tile("gate", [P, PACK, J], F32)
@@ -81,13 +80,9 @@ def tile_list_crossed_tablegate_skip_plain_kernel(
                 queue.dma_start(out=rows[r:P:32, :].bitcast(I32), in_=rows[8 * r : P : 32, :].bitcast(I32))
 
         tg_rows = tg.rearrange("(p t) q -> t p q", t=PACK)
-        nc.gpsimd.memset(planes[:, W_S:].bitcast(I32), 0)
-        nc.vector.memset(planes2[:].bitcast(I32), 0)
+        nc.vector.memset(planes[:, W_S:].bitcast(I32), 0)
         nc.gpsimd.dma_start(out=slope[:], in_=sg.rearrange("(p t) o -> p (t o)", t=PACK))
         nc.gpsimd.dma_start(out=offset[:], in_=bg.rearrange("(p t) o -> p (t o)", t=PACK))
-        load_rows(nc.gpsimd, planes2, WB_S, wb_scales)
-        load_rows(nc.gpsimd, planes2, SX_S, sx_scales)
-        load_rows(nc.gpsimd, planes2, WS_S, ws_scales)
         make_identity(nc, ident[:])
 
         nc.sync.dma_start(list_t[:], offs)
@@ -111,10 +106,16 @@ def tile_list_crossed_tablegate_skip_plain_kernel(
         xt_g = tile("xt_g", [P, J], U16, tag="xo_sg")
         nc.vector.tensor_copy(xt_g[:], xt_tab[:].indirect(list_t[:]))
         nc.vector.tensor_copy(xo_g[:], xo_tab[:].indirect(list_o[:]))
-        for t in range(1, PACK):
-            gate_tab.append(tenant("gate_tab%d" % t, [P, Q], F32, at=4096 * (t - 1)))
-        for t in range(1, PACK):
+        for t, at in ((1, 0), (2, 4864), (3, 8960)):
+            gate_tab.append(tenant("gate_tab%d" % t, [P, Q], F32, at=at))
+        planes2 = tenant("planes2", [P, WIDTH2], U8, at=4096)
+        nc.vector.memset(planes2[:].bitcast(I32), 0)
+        for t in (1, 2):
             nc.sync.dma_start(out=gate_tab[t][:], in_=tg_rows[t])
+        load_rows(nc.sync, planes2, WB_S, wb_scales)
+        load_rows(nc.sync, planes2, SX_S, sx_scales)
+        load_rows(nc.sync, planes2, WS_S, ws_scales)
+        nc.sync.dma_start(out=gate_tab[3][:], in_=tg_rows[3])
 
         acc_a = [ps.tile([P, R], F32, name="acc_a%d" % h) for h in range(halves)]
         acc_b = [ps.tile([P, R], F32, name="acc_b%d" % h) for h in range(halves)]
@@ -140,8 +141,9 @@ def tile_list_crossed_tablegate_skip_plain_kernel(
         for h in range(halves):
             product(acc_a[h], token[h], first, True)
         for h in range(halves):
-            product(acc_b[h], token[h], second, True)
             product(acc_a[h], note[h], second, False)
+        for h in range(halves):
+            product(acc_b[h], token[h], second, True)
             product(acc_b[h], note[h], first, False)
 
         def look(t):
@@ -151,9 +153,9 @@ def tile_list_crossed_tablegate_skip_plain_kernel(
             )
 
         look(0)
-        ws_sb = tenant("ws_sb", [P, N], U32, at=12288)
-        sx_sb = tenant("sx_sb", [P, J], U32, at=12288 + 1024)
-        wb_sb = tenant("wb_sb", [P, 2 * N], U8, at=12288 + 2048)
+        ws_sb = tenant("ws_sb", [P, N], U32, at=13056)
+        sx_sb = tenant("sx_sb", [P, J], U32, at=13056 + 1024)
+        wb_sb = tenant("wb_sb", [P, 2 * N], U8, at=13056 + 2048)
         nc.sync.dma_start(out=ws_sb[:].bitcast(I32), in_=words(ws_words))
         nc.sync.dma_start(out=sx_sb[:].bitcast(I32), in_=words(sx_words))
         nc.sync.dma_start(out=wb_sb[:].bitcast(I32), in_=wb_words[0].bitcast(I32))

@@ -20,7 +20,26 @@ ALU = mybir.AluOpType
 
 P = 128
 PACK = 4
+BLOCK_ROWS = 8
+QUADRANT = 32
 HALF = 128
+HALVES = J // HALF
+N_TILES = N // P
+
+XT_S, XO_S, W_S, W2_S, WIDTH1 = 0, J, 2 * J, 2 * J + R, 2 * J + 2 * R
+WB_S, SX_S, WS_S, WIDTH2 = 0, N, N + J, 2 * N + J
+
+GATE_BYTES = 4 * Q
+GATE1_AT = 0
+PLANES2_AT = GATE1_AT + GATE_BYTES
+GATE2_AT = PLANES2_AT + WIDTH2
+XT_TAB_AT = PLANES2_AT - 512
+GATE3_AT = GATE2_AT + GATE_BYTES
+XO_TAB_AT = GATE3_AT
+GATE0_AT = GATE3_AT + GATE_BYTES
+W2_AT = GATE0_AT + GATE_BYTES
+XT_G_AT = W2_AT + 4 * R
+XO_SG_AT = XT_G_AT - J // 2
 
 
 def tile_list_crossed_tablegate_skip_plain_kernel(
@@ -28,121 +47,117 @@ def tile_list_crossed_tablegate_skip_plain_kernel(
     wb_words, wb_scales, sx_words, sx_scales, ws_words, ws_scales, offs, offs2, offs3, out,
 ):
     nc = tc.nc
-    halves = J // HALF
-
-    def words(dram):
-        return dram[0].rearrange("p c b -> p (c b)").bitcast(I32)
 
     with ExitStack() as ctx:
         sb = ctx.enter_context(tc.tile_pool(name="sb", bufs=1))
         ps = ctx.enter_context(tc.psum_pool(name="ps", bufs=1))
+        reused = ctx.enter_context(tc.tile_pool(name="reused", bufs=1))
 
-        def tile(name, shape, dtype, tag=None):
-            return sb.tile(shape, dtype, name=name, tag=tag or name, align_bytes=64)
+        def tile(name, shape, dtype):
+            return sb.tile(shape, dtype, name=name, align_bytes=64)
 
-        shared = ctx.enter_context(tc.tile_pool(name="shared", bufs=1))
+        def tenant(name, shape, dtype, at):
+            return reused.tile(shape, dtype, name=name, align_bytes=64, offset=at)
 
-        def tenant(name, shape, dtype, at=0):
-            return shared.tile(shape, dtype, name=name, align_bytes=64, offset=at)
+        def load_bytes(into, source):
+            nc.sync.dma_start(out=into.bitcast(I32), in_=source.bitcast(I32))
 
-        XT_S, XO_S, W_S, W2_S, WIDTH = 0, J, 2 * J, 2 * J + R, 2 * J + 2 * R
-        WB_S, SX_S, WS_S, WIDTH2 = 0, N, N + J, 2 * N + J
+        def load_fp8_words(into, words):
+            load_bytes(into[:], words[0].rearrange("p c b -> p (c b)"))
+
+        def load_scale_rows(into, first, scales):
+            load_bytes(into[0:P:BLOCK_ROWS, first : first + scales.shape[2]], scales[0])
+
+        def place_scale_rows(planes_tile):
+            for r in range(1, QUADRANT // BLOCK_ROWS):
+                load_bytes(planes_tile[r:P:QUADRANT, :], planes_tile[BLOCK_ROWS * r : P : QUADRANT, :])
+
+        def half(h, first=0):
+            return slice(first + h * HALF, first + (h + 1) * HALF)
 
         list_t = tile("list_t", [P, J // 16], U16)
         list_o = tile("list_o", [P, J // 16], U16)
         list_g = tile("list_g", [P, J // 16], U16)
-        xt_tab = tenant("xt_tab", [P, T], U16, at=3584)
-        xo_tab = tenant("xo_tab", [P, Z], U32, at=8960)
+        xt_tab = tenant("xt_tab", [P, T], U16, XT_TAB_AT)
+        xo_tab = tenant("xo_tab", [P, Z], U32, XO_TAB_AT)
         xt_stab = tile("xt_stab", [P, T], U8)
         xo_stab = tile("xo_stab", [P, Z], U8)
         xo_g = tile("xo_g", [P, J], U32)
         xt_sg = tile("xt_sg", [P, J], U8)
-        xo_sg = tile("xo_sg", [P, J], U8)
+        xo_sg = tenant("xo_sg", [P, J], U8, XO_SG_AT)
         w_sb = tile("w_sb", [P, R], U32)
-        w2_sb = tile("w2_sb", [P, R], U32)
-        planes = tile("planes", [P, WIDTH], U8)
-        gate_tab = [tenant("gate_tab0", [P, Q], F32, at=13056)]
+        planes = tile("planes", [P, WIDTH1], U8)
+        gate_tab = [tenant("gate_tab0", [P, Q], F32, GATE0_AT)]
         slope = tile("slope", [P, PACK], F32)
         offset = tile("offset", [P, PACK], F32)
         gate = tile("gate", [P, PACK, J], F32)
         ident = tile("ident", [P, P], F32)
-
-        def load_rows(queue, into, first, scales):
-            queue.dma_start(out=into[0:P:8, first : first + scales.shape[2]].bitcast(I32), in_=scales[0].bitcast(I32))
-
-        def load_window(window, scales):
-            rows, width = scales.shape[1], scales.shape[2] // 4
-            source = scales[0].bitcast(I32).unsqueeze(1).to_broadcast([rows, P // rows, width])
-            nc.sync.dma_start(out=window[:].bitcast(I32), in_=source)
-
-        def spread(queue, rows):
-            for r in range(1, 4):
-                queue.dma_start(out=rows[r:P:32, :].bitcast(I32), in_=rows[8 * r : P : 32, :].bitcast(I32))
-
         tg_rows = tg.rearrange("(p t) q -> t p q", t=PACK)
+
+        nc.vector.memset(xo_stab[:].bitcast(I32), 0)
         nc.vector.memset(planes[:, W_S:].bitcast(I32), 0)
         nc.gpsimd.dma_start(out=slope[:], in_=sg.rearrange("(p t) o -> p (t o)", t=PACK))
         nc.gpsimd.dma_start(out=offset[:], in_=bg.rearrange("(p t) o -> p (t o)", t=PACK))
         make_identity(nc, ident[:])
 
+        xt_rows = xt_scales[0].bitcast(I32)
+        nc.sync.dma_start(
+            out=xt_stab[:].bitcast(I32),
+            in_=xt_rows.unsqueeze(1).to_broadcast([xt_rows.shape[0], BLOCK_ROWS, xt_rows.shape[1]]),
+        )
         nc.sync.dma_start(list_t[:], offs)
-        load_window(xt_stab, xt_scales)
         nc.sync.dma_start(list_o[:], offs2)
-        load_window(xo_stab, xo_scales)
-        load_rows(nc.sync, planes, W_S, w_scales)
-        load_rows(nc.sync, planes, W2_S, w2_scales)
-        nc.sync.dma_start(out=xt_tab[:].bitcast(I32), in_=xt_words[0].bitcast(I32))
+        load_scale_rows(xo_stab, 0, xo_scales)
+        load_bytes(xt_tab[:], xt_words[0])
+        load_scale_rows(planes, W_S, w_scales)
+        load_scale_rows(planes, W2_S, w2_scales)
         nc.sync.dma_start(out=gate_tab[0][:], in_=tg_rows[0])
         nc.sync.dma_start(list_g[:], offs3)
-        nc.sync.dma_start(out=w_sb[:].bitcast(I32), in_=words(w_words))
-        nc.sync.dma_start(out=xo_tab[:].bitcast(I32), in_=words(xo_words))
-        nc.sync.dma_start(out=w2_sb[:].bitcast(I32), in_=words(w2_words))
+        load_fp8_words(w_sb, w_words)
+        load_fp8_words(xo_tab, xo_words)
 
         nc.vector.tensor_copy(xt_sg[:], xt_stab[:].indirect(list_t[:]))
         nc.vector.tensor_copy(xo_sg[:], xo_stab[:].indirect(list_o[:]))
         nc.vector.tensor_copy(planes[:, XT_S : XT_S + J].bitcast(I32), xt_sg[:].bitcast(I32))
         nc.vector.tensor_copy(planes[:, XO_S : XO_S + J].bitcast(I32), xo_sg[:].bitcast(I32))
-        spread(nc.scalar, planes)
-        xt_g = tile("xt_g", [P, J], U16, tag="xo_sg")
+        place_scale_rows(planes)
+        w2_sb = tenant("w2_sb", [P, R], U32, W2_AT)
+        load_fp8_words(w2_sb, w2_words)
+        xt_g = tenant("xt_g", [P, J], U16, XT_G_AT)
         nc.vector.tensor_copy(xt_g[:], xt_tab[:].indirect(list_t[:]))
         nc.vector.tensor_copy(xo_g[:], xo_tab[:].indirect(list_o[:]))
-        for t, at in ((1, 0), (2, 4864), (3, 8960)):
-            gate_tab.append(tenant("gate_tab%d" % t, [P, Q], F32, at=at))
-        planes2 = tenant("planes2", [P, WIDTH2], U8, at=4096)
+
+        for t, at in ((1, GATE1_AT), (2, GATE2_AT), (3, GATE3_AT)):
+            gate_tab.append(tenant("gate_tab%d" % t, [P, Q], F32, at))
+        planes2 = tenant("planes2", [P, WIDTH2], U8, PLANES2_AT)
         nc.vector.memset(planes2[:].bitcast(I32), 0)
         for t in (1, 2):
             nc.sync.dma_start(out=gate_tab[t][:], in_=tg_rows[t])
-        load_rows(nc.sync, planes2, WB_S, wb_scales)
-        load_rows(nc.sync, planes2, SX_S, sx_scales)
-        load_rows(nc.sync, planes2, WS_S, ws_scales)
+        load_scale_rows(planes2, WB_S, wb_scales)
+        load_scale_rows(planes2, SX_S, sx_scales)
+        load_scale_rows(planes2, WS_S, ws_scales)
         nc.sync.dma_start(out=gate_tab[3][:], in_=tg_rows[3])
 
-        acc_a = [ps.tile([P, R], F32, name="acc_a%d" % h) for h in range(halves)]
-        acc_b = [ps.tile([P, R], F32, name="acc_b%d" % h) for h in range(halves)]
-        turned = [ps.tile([P, PACK, HALF], F32, name="turned%d" % h) for h in range(halves)]
+        acc_a = [ps.tile([P, R], F32, name="acc_a%d" % h) for h in range(HALVES)]
+        acc_b = [ps.tile([P, R], F32, name="acc_b%d" % h) for h in range(HALVES)]
+        turned = [ps.tile([P, PACK, HALF], F32, name="turned%d" % h) for h in range(HALVES)]
 
         first = (w_sb[:].bitcast(E4M3), planes[:, W_S : W_S + R])
         second = (w2_sb[:].bitcast(E5M2), planes[:, W2_S : W2_S + R])
-        token = [
-            (xt_g[:, h * HALF : (h + 1) * HALF].bitcast(E2M1), planes[:, XT_S + h * HALF : XT_S + (h + 1) * HALF])
-            for h in range(halves)
-        ]
-        note = [
-            (xo_g[:, h * HALF : (h + 1) * HALF].bitcast(E4M3), planes[:, XO_S + h * HALF : XO_S + (h + 1) * HALF])
-            for h in range(halves)
-        ]
+        token = [(xt_g[:, half(h)].bitcast(E2M1), planes[:, half(h, XT_S)]) for h in range(HALVES)]
+        note = [(xo_g[:, half(h)].bitcast(E4M3), planes[:, half(h, XO_S)]) for h in range(HALVES)]
 
-        def product(acc, slots, weight, opens):
+        def product(acc, stationary, moving, opens):
             nc.tensor.matmul_mx(
-                out=acc[:], lhsT=slots[0], lhsT_scale=slots[1], rhs=weight[0], rhs_scale=weight[1],
+                out=acc[:], lhsT=stationary[0], lhsT_scale=stationary[1], rhs=moving[0], rhs_scale=moving[1],
                 start=opens, stop=not opens,
             )
 
-        for h in range(halves):
+        for h in range(HALVES):
             product(acc_a[h], token[h], first, True)
-        for h in range(halves):
+        for h in range(HALVES):
             product(acc_a[h], note[h], second, False)
-        for h in range(halves):
+        for h in range(HALVES):
             product(acc_b[h], token[h], second, True)
             product(acc_b[h], note[h], first, False)
 
@@ -153,21 +168,22 @@ def tile_list_crossed_tablegate_skip_plain_kernel(
             )
 
         look(0)
-        ws_sb = tenant("ws_sb", [P, N], U32, at=13056)
-        sx_sb = tenant("sx_sb", [P, J], U32, at=13056 + 1024)
-        wb_sb = tenant("wb_sb", [P, 2 * N], U8, at=13056 + 2048)
-        nc.sync.dma_start(out=ws_sb[:].bitcast(I32), in_=words(ws_words))
-        nc.sync.dma_start(out=sx_sb[:].bitcast(I32), in_=words(sx_words))
-        nc.sync.dma_start(out=wb_sb[:].bitcast(I32), in_=wb_words[0].bitcast(I32))
-        spread(nc.sync, planes2)
+        ws_sb = tenant("ws_sb", [P, N], U32, GATE0_AT)
+        sx_sb = tenant("sx_sb", [P, J], U32, GATE0_AT + 4 * N)
+        wb_sb = tenant("wb_sb", [P, 2 * N], U8, GATE0_AT + 4 * N + 4 * J)
+        load_fp8_words(ws_sb, ws_words)
+        load_fp8_words(sx_sb, sx_words)
+        load_bytes(wb_sb[:], wb_words[0])
+        place_scale_rows(planes2)
         look(1)
-        a_sb = [sb.tile([P, PACK, P], F32, name="a_sb%d" % h) for h in range(halves)]
-        larger = [sb.tile([P, PACK, P], F32, name="larger%d" % h) for h in range(halves)]
-        for h in range(halves):
+        a_sb = [sb.tile([P, PACK, P], F32, name="a_sb%d" % h) for h in range(HALVES)]
+        larger = [sb.tile([P, PACK, P], F32, name="larger%d" % h) for h in range(HALVES)]
+        for h in range(HALVES):
             nc.scalar.copy(out=a_sb[h][:], in_=acc_a[h][:].rearrange("j (p t) -> j t p", t=PACK))
         look(2)
         look(3)
-        for h in range(halves):
+
+        for h in range(HALVES):
             b_rows = acc_b[h][:].rearrange("j (p t) -> j t p", t=PACK)
             for pair in range(0, PACK, 2):
                 nc.vector.tensor_tensor(
@@ -178,46 +194,38 @@ def tile_list_crossed_tablegate_skip_plain_kernel(
                 nc.tensor.transpose(turned[h][:, t, :], larger[h][:, t, :], ident[:])
 
         acc_y = [
-            [ps.tile([P, HALF], F32, name="acc_y0%d" % u) for u in range(N // P)],
-            [ps.tile([P, HALF], F32, name="acc_y1%d" % u, tag="acc_a%d" % u) for u in range(N // P)],
+            [ps.tile([P, HALF], F32, name="acc_y0%d" % u) for u in range(N_TILES)],
+            [ps.tile([P, HALF], F32, name="acc_y1%d" % u, tag="acc_a%d" % u) for u in range(N_TILES)],
         ]
-        for h in range(halves):
-            for u in range(N // P):
-                nc.tensor.matmul_mx(
-                    out=acc_y[h][u][:], lhsT=ws_sb[:, u * P : (u + 1) * P].bitcast(E4M3),
-                    lhsT_scale=planes2[:, WS_S + u * P : WS_S + (u + 1) * P],
-                    rhs=sx_sb[:, h * HALF : (h + 1) * HALF].bitcast(E4M3),
-                    rhs_scale=planes2[:, SX_S + h * HALF : SX_S + (h + 1) * HALF], start=True, stop=False,
-                )
+        for h in range(HALVES):
+            own = (sx_sb[:, half(h)].bitcast(E4M3), planes2[:, half(h, SX_S)])
+            for u in range(N_TILES):
+                rows = slice(u * P, (u + 1) * P)
+                product(acc_y[h][u], (ws_sb[:, rows].bitcast(E4M3), planes2[:, WS_S + u * P : WS_S + (u + 1) * P]), own, True)
 
-        hid = [sb.tile([P, HALF, PACK], BF16, name="hid%d" % h, align_bytes=64) for h in range(halves)]
-        hid_q = [sb.tile([P, HALF], U32, name="hid_q%d" % h, align_bytes=64) for h in range(halves)]
-        hid_s = [sb.tile([P, HALF], U8, name="hid_s%d" % h, align_bytes=64) for h in range(halves)]
-        for h in range(halves):
+        hid = [tile("hid%d" % h, [P, HALF, PACK], BF16) for h in range(HALVES)]
+        hid_q = [tile("hid_q%d" % h, [P, HALF], U32) for h in range(HALVES)]
+        hid_s = [tile("hid_s%d" % h, [P, HALF], U8) for h in range(HALVES)]
+        for h in range(HALVES):
             nc.vector.tensor_tensor(
                 out=hid[h][:], in0=turned[h][:].rearrange("p t j -> p j t"),
-                in1=gate[:, :, h * HALF : (h + 1) * HALF].rearrange("p t j -> p j t"), op=ALU.mult,
+                in1=gate[:, :, half(h)].rearrange("p t j -> p j t"), op=ALU.mult,
             )
-        for h in range(halves):
+        for h in range(HALVES):
             nc.vector.quantize_mx(
                 out=hid_q[h][:].bitcast(E5M2), scales=hid_s[h][:], in_=hid[h][:].rearrange("p j t -> p (j t)")
             )
-            for u in range(N // P):
-                nc.tensor.matmul_mx(
-                    out=acc_y[h][u][:],
-                    lhsT=wb_sb[:, 2 * u * P : 2 * (u + 1) * P].bitcast(E2M1),
-                    lhsT_scale=planes2[:, WB_S + u * P : WB_S + (u + 1) * P],
-                    rhs=hid_q[h][:].bitcast(E5M2), rhs_scale=hid_s[h][:], start=False, stop=True,
-                )
+            for u in range(N_TILES):
+                weight = (wb_sb[:, 2 * u * P : 2 * (u + 1) * P].bitcast(E2M1), planes2[:, WB_S + u * P : WB_S + (u + 1) * P])
+                product(acc_y[h][u], weight, (hid_q[h][:].bitcast(E5M2), hid_s[h][:]), False)
 
-        for h in range(halves):
-            cols = slice(h * HALF, (h + 1) * HALF)
+        for h in range(HALVES):
             y_top = sb.tile([P, HALF], F32, name="y_top%d" % h)
             nc.scalar.copy(out=y_top[:], in_=acc_y[h][0][:])
-            nc.scalar.dma_start(out=out[0:P, cols], in_=y_top[:])
+            nc.scalar.dma_start(out=out[0:P, half(h)], in_=y_top[:])
             y_low = sb.tile([P, HALF], F32, name="y_low%d" % h)
-            if h == halves - 1:
+            if h == HALVES - 1:
                 nc.vector.tensor_copy(out=y_low[:], in_=acc_y[h][1][:])
             else:
                 nc.scalar.copy(out=y_low[:], in_=acc_y[h][1][:])
-            nc.sync.dma_start(out=out[P : 2 * P, cols], in_=y_low[:])
+            nc.sync.dma_start(out=out[P : 2 * P, half(h)], in_=y_low[:])

from contextlib import ExitStack

import concourse.mybir as mybir
from concourse.masks import make_identity

K, T, Z, J, R, Q, N, L = 512, 1024, 1024, 256, 512, 1024, 256, 512
FLOPS = 2 * (4 * K * R * J + R * N * J + L * N * J)

F32 = mybir.dt.float32
BF16 = mybir.dt.bfloat16
I32 = mybir.dt.int32
U32 = mybir.dt.uint32
U16 = mybir.dt.uint16
U8 = mybir.dt.uint8
E4M3 = mybir.dt.float8_e4m3fn_x4
E5M2 = mybir.dt.float8_e5m2_x4
E2M1 = mybir.dt.float4_e2m1fn_x4
ACT = mybir.ActivationFunctionType
ALU = mybir.AluOpType

P = 128
PACK = 4
BLOCK_ROWS = 8
QUADRANT = 32
HALF = 128
HALVES = J // HALF
N_TILES = N // P

XT_S, XO_S, W_S, W2_S, WIDTH1 = 0, J, 2 * J, 2 * J + R, 2 * J + 2 * R
WB_S, SX_S, WS_S, WIDTH2 = 0, N, N + J, 2 * N + J

GATE_BYTES = 4 * Q
GATE1_AT = 0
PLANES2_AT = GATE1_AT + GATE_BYTES
GATE2_AT = PLANES2_AT + WIDTH2
XT_TAB_AT = PLANES2_AT - 512
GATE3_AT = GATE2_AT + GATE_BYTES
XO_TAB_AT = GATE3_AT
GATE0_AT = GATE3_AT + GATE_BYTES
W2_AT = GATE0_AT + GATE_BYTES
XT_G_AT = W2_AT + 4 * R
XO_SG_AT = XT_G_AT - J // 2


def tile_list_crossed_tablegate_skip_plain_kernel(
    tc, xt_words, xt_scales, xo_words, xo_scales, w_words, w_scales, w2_words, w2_scales, tg, sg, bg,
    wb_words, wb_scales, sx_words, sx_scales, ws_words, ws_scales, offs, offs2, offs3, out,
):
    nc = tc.nc

    with ExitStack() as ctx:
        sb = ctx.enter_context(tc.tile_pool(name="sb", bufs=1))
        ps = ctx.enter_context(tc.psum_pool(name="ps", bufs=1))
        reused = ctx.enter_context(tc.tile_pool(name="reused", bufs=1))

        def tile(name, shape, dtype):
            return sb.tile(shape, dtype, name=name, align_bytes=64)

        def tenant(name, shape, dtype, at):
            return reused.tile(shape, dtype, name=name, align_bytes=64, offset=at)

        def load_bytes(into, source):
            nc.sync.dma_start(out=into.bitcast(I32), in_=source.bitcast(I32))

        def load_fp8_words(into, words):
            load_bytes(into[:], words[0].rearrange("p c b -> p (c b)"))

        def load_scale_rows(into, first, scales):
            load_bytes(into[0:P:BLOCK_ROWS, first : first + scales.shape[2]], scales[0])

        def place_scale_rows(planes_tile):
            for r in range(1, QUADRANT // BLOCK_ROWS):
                load_bytes(planes_tile[r:P:QUADRANT, :], planes_tile[BLOCK_ROWS * r : P : QUADRANT, :])

        def half(h, first=0):
            return slice(first + h * HALF, first + (h + 1) * HALF)

        list_t = tile("list_t", [P, J // 16], U16)
        list_o = tile("list_o", [P, J // 16], U16)
        list_g = tile("list_g", [P, J // 16], U16)
        xt_tab = tenant("xt_tab", [P, T], U16, XT_TAB_AT)
        xo_tab = tenant("xo_tab", [P, Z], U32, XO_TAB_AT)
        xt_stab = tile("xt_stab", [P, T], U8)
        xo_stab = tile("xo_stab", [P, Z], U8)
        xo_g = tile("xo_g", [P, J], U32)
        xt_sg = tile("xt_sg", [P, J], U8)
        xo_sg = tenant("xo_sg", [P, J], U8, XO_SG_AT)
        w_sb = tile("w_sb", [P, R], U32)
        planes = tile("planes", [P, WIDTH1], U8)
        gate_tab = [tenant("gate_tab0", [P, Q], F32, GATE0_AT)]
        slope = tile("slope", [P, PACK], F32)
        offset = tile("offset", [P, PACK], F32)
        gate = tile("gate", [P, PACK, J], F32)
        ident = tile("ident", [P, P], F32)
        tg_rows = tg.rearrange("(p t) q -> t p q", t=PACK)

        nc.vector.memset(xo_stab[:].bitcast(I32), 0)
        nc.vector.memset(planes[:, W_S:].bitcast(I32), 0)
        nc.gpsimd.dma_start(out=slope[:], in_=sg.rearrange("(p t) o -> p (t o)", t=PACK))
        nc.gpsimd.dma_start(out=offset[:], in_=bg.rearrange("(p t) o -> p (t o)", t=PACK))
        make_identity(nc, ident[:])

        xt_rows = xt_scales[0].bitcast(I32)
        nc.sync.dma_start(
            out=xt_stab[:].bitcast(I32),
            in_=xt_rows.unsqueeze(1).to_broadcast([xt_rows.shape[0], BLOCK_ROWS, xt_rows.shape[1]]),
        )
        nc.sync.dma_start(list_t[:], offs)
        nc.sync.dma_start(list_o[:], offs2)
        load_scale_rows(xo_stab, 0, xo_scales)
        load_bytes(xt_tab[:], xt_words[0])
        load_scale_rows(planes, W_S, w_scales)
        load_scale_rows(planes, W2_S, w2_scales)
        nc.sync.dma_start(out=gate_tab[0][:], in_=tg_rows[0])
        nc.sync.dma_start(list_g[:], offs3)
        load_fp8_words(w_sb, w_words)
        load_fp8_words(xo_tab, xo_words)

        nc.vector.tensor_copy(xt_sg[:], xt_stab[:].indirect(list_t[:]))
        nc.vector.tensor_copy(xo_sg[:], xo_stab[:].indirect(list_o[:]))
        nc.vector.tensor_copy(planes[:, XT_S : XT_S + J].bitcast(I32), xt_sg[:].bitcast(I32))
        nc.vector.tensor_copy(planes[:, XO_S : XO_S + J].bitcast(I32), xo_sg[:].bitcast(I32))
        place_scale_rows(planes)
        w2_sb = tenant("w2_sb", [P, R], U32, W2_AT)
        load_fp8_words(w2_sb, w2_words)
        xt_g = tenant("xt_g", [P, J], U16, XT_G_AT)
        nc.vector.tensor_copy(xt_g[:], xt_tab[:].indirect(list_t[:]))
        nc.vector.tensor_copy(xo_g[:], xo_tab[:].indirect(list_o[:]))

        for t, at in ((1, GATE1_AT), (2, GATE2_AT), (3, GATE3_AT)):
            gate_tab.append(tenant("gate_tab%d" % t, [P, Q], F32, at))
        planes2 = tenant("planes2", [P, WIDTH2], U8, PLANES2_AT)
        nc.vector.memset(planes2[:].bitcast(I32), 0)
        for t in (1, 2):
            nc.sync.dma_start(out=gate_tab[t][:], in_=tg_rows[t])
        load_scale_rows(planes2, WB_S, wb_scales)
        load_scale_rows(planes2, SX_S, sx_scales)
        load_scale_rows(planes2, WS_S, ws_scales)
        nc.sync.dma_start(out=gate_tab[3][:], in_=tg_rows[3])

        acc_a = [ps.tile([P, R], F32, name="acc_a%d" % h) for h in range(HALVES)]
        acc_b = [ps.tile([P, R], F32, name="acc_b%d" % h) for h in range(HALVES)]
        turned = [ps.tile([P, PACK, HALF], F32, name="turned%d" % h) for h in range(HALVES)]

        first = (w_sb[:].bitcast(E4M3), planes[:, W_S : W_S + R])
        second = (w2_sb[:].bitcast(E5M2), planes[:, W2_S : W2_S + R])
        token = [(xt_g[:, half(h)].bitcast(E2M1), planes[:, half(h, XT_S)]) for h in range(HALVES)]
        note = [(xo_g[:, half(h)].bitcast(E4M3), planes[:, half(h, XO_S)]) for h in range(HALVES)]

        def product(acc, stationary, moving, opens):
            nc.tensor.matmul_mx(
                out=acc[:], lhsT=stationary[0], lhsT_scale=stationary[1], rhs=moving[0], rhs_scale=moving[1],
                start=opens, stop=not opens,
            )

        for h in range(HALVES):
            product(acc_a[h], token[h], first, True)
        for h in range(HALVES):
            product(acc_a[h], note[h], second, False)
        for h in range(HALVES):
            product(acc_b[h], token[h], second, True)
            product(acc_b[h], note[h], first, False)

        def look(t):
            nc.scalar.activation(
                out=gate[:, t, :], in_=gate_tab[t][:].indirect(list_g[:]), func=ACT.Sigmoid,
                bias=offset[:, t : t + 1], scale=slope[:, t : t + 1],
            )

        look(0)
        ws_sb = tenant("ws_sb", [P, N], U32, GATE0_AT)
        sx_sb = tenant("sx_sb", [P, J], U32, GATE0_AT + 4 * N)
        wb_sb = tenant("wb_sb", [P, 2 * N], U8, GATE0_AT + 4 * N + 4 * J)
        load_fp8_words(ws_sb, ws_words)
        load_fp8_words(sx_sb, sx_words)
        load_bytes(wb_sb[:], wb_words[0])
        place_scale_rows(planes2)
        look(1)
        a_sb = [sb.tile([P, PACK, P], F32, name="a_sb%d" % h) for h in range(HALVES)]
        larger = [sb.tile([P, PACK, P], F32, name="larger%d" % h) for h in range(HALVES)]
        for h in range(HALVES):
            nc.scalar.copy(out=a_sb[h][:], in_=acc_a[h][:].rearrange("j (p t) -> j t p", t=PACK))
        look(2)
        look(3)

        for h in range(HALVES):
            b_rows = acc_b[h][:].rearrange("j (p t) -> j t p", t=PACK)
            for pair in range(0, PACK, 2):
                nc.vector.tensor_tensor(
                    out=larger[h][:, pair : pair + 2, :], in0=b_rows[:, pair : pair + 2, :],
                    in1=a_sb[h][:, pair : pair + 2, :], op=ALU.max,
                )
            for t in range(PACK):
                nc.tensor.transpose(turned[h][:, t, :], larger[h][:, t, :], ident[:])

        acc_y = [
            [ps.tile([P, HALF], F32, name="acc_y0%d" % u) for u in range(N_TILES)],
            [ps.tile([P, HALF], F32, name="acc_y1%d" % u, tag="acc_a%d" % u) for u in range(N_TILES)],
        ]
        for h in range(HALVES):
            own = (sx_sb[:, half(h)].bitcast(E4M3), planes2[:, half(h, SX_S)])
            for u in range(N_TILES):
                rows = slice(u * P, (u + 1) * P)
                product(acc_y[h][u], (ws_sb[:, rows].bitcast(E4M3), planes2[:, WS_S + u * P : WS_S + (u + 1) * P]), own, True)

        hid = [tile("hid%d" % h, [P, HALF, PACK], BF16) for h in range(HALVES)]
        hid_q = [tile("hid_q%d" % h, [P, HALF], U32) for h in range(HALVES)]
        hid_s = [tile("hid_s%d" % h, [P, HALF], U8) for h in range(HALVES)]
        for h in range(HALVES):
            nc.vector.tensor_tensor(
                out=hid[h][:], in0=turned[h][:].rearrange("p t j -> p j t"),
                in1=gate[:, :, half(h)].rearrange("p t j -> p j t"), op=ALU.mult,
            )
        for h in range(HALVES):
            nc.vector.quantize_mx(
                out=hid_q[h][:].bitcast(E5M2), scales=hid_s[h][:], in_=hid[h][:].rearrange("p j t -> p (j t)")
            )
            for u in range(N_TILES):
                weight = (wb_sb[:, 2 * u * P : 2 * (u + 1) * P].bitcast(E2M1), planes2[:, WB_S + u * P : WB_S + (u + 1) * P])
                product(acc_y[h][u], weight, (hid_q[h][:].bitcast(E5M2), hid_s[h][:]), False)

        for h in range(HALVES):
            y_top = sb.tile([P, HALF], F32, name="y_top%d" % h)
            nc.scalar.copy(out=y_top[:], in_=acc_y[h][0][:])
            nc.scalar.dma_start(out=out[0:P, half(h)], in_=y_top[:])
            y_low = sb.tile([P, HALF], F32, name="y_low%d" % h)
            if h == HALVES - 1:
                nc.vector.tensor_copy(out=y_low[:], in_=acc_y[h][1][:])
            else:
                nc.scalar.copy(out=y_low[:], in_=acc_y[h][1][:])
            nc.sync.dma_start(out=out[P : 2 * P, half(h)], in_=y_low[:])
